import numpy as np
import ml_dtypes


def mxq(x, axis, fmt="e4m3"):
    dtype, down = {"e4m3": (ml_dtypes.float8_e4m3fn, 7), "e5m2": (ml_dtypes.float8_e5m2, 14)}[fmt]
    v = np.moveaxis(np.asarray(x, np.float32).astype(ml_dtypes.bfloat16).astype(np.float64), axis, -1)
    blocks = v.reshape(v.shape[:-1] + (-1, 32))
    amax = np.abs(blocks).max(-1, keepdims=True)
    byte = np.maximum(np.where(amax > 0, np.frexp(amax)[1] - 1 + 127, 0) - down, 1)
    scale = np.exp2(byte - 127.0)
    codes = (blocks / scale).astype(np.float32).astype(dtype).astype(np.float64)
    return np.moveaxis((codes * scale).reshape(v.shape), -1, axis)


WIDE = False


def mx_kscale(k):
    if not WIDE:
        return np.ones(k)
    levels = np.array([10, -10, 5, -5, 0])
    if k % 512:
        return np.exp2(np.random.permutation(np.resize(levels, k // 32))).repeat(32)
    a = np.empty((k // 512, 16))
    for p in range(k // 512):
        a[p, :8] = np.random.permutation(np.resize(levels, 8))
        for g in range(8):
            far = levels[np.abs(levels - a[p, g]) >= 10]
            a[p, g + 8] = far[np.random.randint(len(far))]
    return np.exp2(a.ravel()).repeat(32)


def f64(x):
    return np.asarray(x).astype(np.float64)


def striped(idx):
    return np.tile(np.asarray(idx).reshape(-1, 16).T, (8, 1)).astype(np.uint16)


def unstriped(offs):
    return offs[:16].T.reshape(-1).astype(np.int64)


E2M1 = np.array([0.0, 0.5, 1.0, 1.5, 2.0, 3.0, 4.0, 6.0, -0.0, -0.5, -1.0, -1.5, -2.0, -3.0, -4.0, -6.0])


def pack_weight(w, fmt):
    k, n = w.shape
    w = f64(np.asarray(w, np.float32).astype(ml_dtypes.bfloat16)).reshape(k // 32, 32, n)
    amax = np.abs(w).max(1)
    if fmt == "e4m3":
        byte = np.frexp(amax)[1] - 1 + 127 - 7
    else:
        mant, ex = np.frexp(amax / 6.0)
        byte = np.where(mant > 0.5, ex, ex - 1) + 127
    byte = np.clip(np.where(amax > 0, byte, 1), 1, 254)
    scaled = (w * np.exp2(127.0 - byte)[:, None, :]).reshape(k, n).astype(np.float32)
    by_word = np.ascontiguousarray(scaled.reshape(k // 512, 128, 4, n).transpose(0, 1, 3, 2))
    if fmt == "e4m3":
        words = by_word.astype(ml_dtypes.float8_e4m3fn).view(np.uint8)
    else:
        c = by_word.astype(ml_dtypes.float4_e2m1fn).view(np.uint8) & 0xF
        words = (c[..., 0::2] | (c[..., 1::2] << 4)).reshape(k // 512, 128, 2 * n)
    return np.ascontiguousarray(words), np.ascontiguousarray(byte.astype(np.uint8).reshape(k // 512, 16, n))


def unpack_weight(words, scales, fmt):
    g, _, n = scales.shape
    words = np.ascontiguousarray(words).reshape(g, 128, n, -1)
    if fmt == "e4m3":
        vals = words.view(ml_dtypes.float8_e4m3fn).astype(np.float64)
    else:
        nib = np.empty((g, 128, n, 4), np.uint8)
        nib[..., 0::2] = words & 0xF
        nib[..., 1::2] = words >> 4
        vals = E2M1[nib]
    vals = vals * np.repeat(np.exp2(scales.astype(np.float64) - 127.0), 8, axis=1)[..., None]
    return vals.transpose(0, 1, 3, 2).reshape(g * 512, n)


def bf(x):
    return np.asarray(x, np.float32).astype(ml_dtypes.bfloat16)


def planes(Y):
    r, m = Y.shape
    b = f64(bf(Y)).reshape(r // 32, 32, m)
    amax = np.abs(b).max(1)
    byte = np.clip(np.where(amax > 0, np.frexp(amax)[1] - 1 + 127 - 7, 1), 1, 254)
    codes = (b * np.exp2(127.0 - byte)[:, None, :]).reshape(r, m).astype(np.float32).astype(ml_dtypes.float8_e4m3fn).view(np.uint8)
    words = codes.reshape(r // 512, 128, 4, m).transpose(0, 1, 3, 2)
    return np.ascontiguousarray(words), np.ascontiguousarray(byte.astype(np.uint8).reshape(r // 512, 16, m))


B, N, T, D, NQ = 1, 512, 2048, 1024, 512


def setup_inputs():
    n = np.random.standard_normal
    pages = np.random.permutation(T // 32)[:B * N // 32]
    idx = (pages[:, None] * 32 + np.arange(32)[None, :]).reshape(-1)
    s = mx_kscale(D)[:, None]
    kp = pack_weight(n((D, T)) / s, "e2m1")
    return {
        "qT": (n((B, D, NQ)) * s * (1.00 / np.sqrt(D))).astype(np.float32),
        "k_words": np.ascontiguousarray(kp[0].reshape(1, 2, 128, T, 2).transpose(0, 2, 3, 1, 4)).reshape(1, 128, T, 4),
        "k_scales": kp[1],
        "ls": (np.random.uniform(7.8, 8.4, (B, 1, NQ))).astype(np.float32),
        "offs": striped(idx),
    }


def reference(qT, k_words, k_scales, ls, offs):
    idx = unstriped(offs)
    pick = lambda x, which: x[:, which].reshape(x.shape[0], B, -1).transpose(1, 0, 2)
    k = unpack_weight(k_words.reshape(1, 128, T, 2, 2).transpose(0, 3, 1, 2, 4).reshape(2, 128, 2 * T), k_scales, "e2m1")
    kg = pick(k, idx)
    qq = mxq(f64(qT), 1, "e4m3")
    a = kg.transpose(0, 2, 1) @ qq
    y = np.exp(a - f64(ls))
    Y = y[0]
    words, scales = planes(Y)
    return Y, words, scales

@@ -1,0 +1,175 @@
+from contextlib import ExitStack
+
+import concourse.mybir as mybir
+from concourse.masks import make_identity
+
+F32 = mybir.dt.float32
+BF16 = mybir.dt.bfloat16
+I32 = mybir.dt.int32
+U32 = mybir.dt.uint32
+U16 = mybir.dt.uint16
+U8 = mybir.dt.uint8
+FP8X4 = mybir.dt.float8_e4m3fn_x4
+FP4X4 = mybir.dt.float4_e2m1fn_x4
+ACT = mybir.ActivationFunctionType
+ALU = mybir.AluOpType
+
+P = 128
+PACK = 4
+PASSES = 2
+SLOTS = 512
+POOL = 2048
+QUERIES = 512
+UNIT = 128
+CHUNK = 256
+FLOPS = 2 * PASSES * P * PACK * SLOTS * QUERIES
+
+
+def interleave(copy, dst, src):
+    copy(
+        dst.rearrange("p (c i) t -> p c t i", i=4),
+        src.rearrange("p t (c i) -> p c t i", i=4),
+    )
+
+
+def tile_attend_plw_soft_kernel(tc, qT, k_words, k_scales, ls, offs, out_0, out_1, out_2):
+    nc = tc.nc
+    with ExitStack() as ctx:
+        keep = ctx.enter_context(tc.tile_pool(name="keep", bufs=1))
+        psum = ctx.enter_context(tc.psum_pool(name="psum", bufs=1))
+
+        offsets = keep.tile([P, SLOTS // 16], U16, name="offsets")
+        nc.sync.dma_start(offsets[:], offs)
+
+        ls_cols = keep.tile([P, 4], F32, name="ls_cols")
+        nc.sync.dma_start(ls_cols[:], ls[0, 0].rearrange("(p j) -> p j", j=4))
+
+        scale_pool = keep.tile([P, POOL], U8, name="scale_pool", align_bytes=64)
+        nc.vector.memset(scale_pool[:].bitcast(I32), 0)
+        scale_rows = k_scales.bitcast(I32).rearrange("o (a i) t -> i a o t", i=4)
+        for i in range(4):
+            nc.sync.dma_start(scale_pool[:].bitcast(I32)[i:P:16, :], scale_rows[i])
+
+        def load_q(chunk, o, tag):
+            raw = keep.tile([P, PACK, CHUNK], F32, name="q_raw_%d_%d" % (chunk, o), tag=tag, align_bytes=64)
+            rows = qT[0, o * P * PACK : (o + 1) * P * PACK, chunk * CHUNK : (chunk + 1) * CHUNK]
+            nc.sync.dma_start(raw[:], rows.rearrange("(p j) w -> p j w", j=PACK))
+            return raw
+
+        q_raw = {}
+        q_raw[0, 0] = load_q(0, 0, "q_first")
+        word_pool = keep.tile([P, POOL], I32, name="word_pool", align_bytes=64)
+        nc.sync.dma_start(word_pool[:], k_words[0].rearrange("p t b -> p (t b)").bitcast(I32))
+        q_raw[0, 1] = load_q(0, 1, "q_second")
+        q_raw[1, 0] = load_q(1, 0, "q_third")
+        q_raw[1, 1] = load_q(1, 1, "q_fourth")
+
+        ident = keep.tile([P, P], F32, name="ident")
+        make_identity(nc, ident[:])
+        ls_bank = psum.tile([P, 4, P], F32, name="ls_bank")
+        for j in range(4):
+            nc.tensor.transpose(ls_bank[:, j, :], ls_cols[:, j : j + 1].to_broadcast([P, P]), ident[:])
+        ls_rows = keep.tile([P, QUERIES], F32, name="ls_rows")
+        nc.scalar.activation(
+            ls_rows[:].rearrange("p (n j) -> p n j", j=4), ls_bank[:].rearrange("p j n -> p n j"), ACT.Copy
+        )
+
+        on_vector = {(2, 1)}
+
+        def scalar_cast(dst, src):
+            nc.scalar.activation(dst, src, ACT.Copy)
+
+        def quantise_q(u, o):
+            chunk, part = divmod(u, CHUNK // UNIT)
+            grouped = keep.tile([P, UNIT, PACK], BF16, name="q_grouped_%d_%d" % (u, o), align_bytes=64)
+            copy = nc.vector.tensor_copy if (u, o) in on_vector else scalar_cast
+            interleave(copy, grouped[:], q_raw[chunk, o][:, :, part * UNIT : (part + 1) * UNIT])
+            codes = keep.tile([P, UNIT], U32, name="q_code_%d_%d" % (u, o), align_bytes=64)
+            scale = keep.tile([P, UNIT], U8, name="q_scale_%d_%d" % (u, o), align_bytes=64)
+            nc.vector.quantize_mx(
+                out=codes[:].bitcast(FP8X4), scales=scale[:], in_=grouped[:].rearrange("p w t -> p (w t)")
+            )
+            return codes, scale
+
+        q_ops = {(u, 0): quantise_q(u, 0) for u in range(CHUNK // UNIT)}
+
+        scales_listed = keep.tile([P, SLOTS], U8, name="scales_listed", align_bytes=64)
+        nc.vector.tensor_copy(scales_listed[:], scale_pool[:].indirect(offsets[:]))
+        k_scale = [
+            keep.tile([P, SLOTS], U8, name="k_scale_0", tag="q_first", align_bytes=64),
+            keep.tile([P, SLOTS], U8, name="k_scale_1", align_bytes=64),
+        ]
+        nc.vector.tensor_copy(
+            k_scale[0][:].rearrange("p (r c i) -> p c r i", r=PACK, i=16),
+            scales_listed[:].rearrange("p (c i r) -> p c r i", r=PACK, i=16),
+        )
+        nc.gpsimd.memset(k_scale[1][:].bitcast(I32), 0)
+        for i in range(4):
+            nc.scalar.dma_start(k_scale[1][:].bitcast(I32)[i:P:32, :], k_scale[0][:].bitcast(I32)[16 + i : P : 32, :])
+
+        words_listed = keep.tile([P, SLOTS], U32, name="words_listed", align_bytes=64)
+        nc.vector.tensor_copy(words_listed[:], word_pool[:].bitcast(U32).indirect(offsets[:]))
+        k_code = []
+        for o in range(PASSES):
+            codes = keep.tile([P, 2 * SLOTS], U8, name="k_code_%d" % o, align_bytes=64)
+            nc.vector.tensor_copy(
+                codes[:].bitcast(U16).rearrange("p (r c i) -> p c r i", r=PACK, i=4),
+                words_listed[:].bitcast(U16).rearrange("p (c i r h) -> p h c r i", r=PACK, i=4, h=PASSES)[:, o],
+            )
+            k_code.append(codes)
+
+
+        y_words = keep.tile([P, QUERIES], I32, name="y_words", align_bytes=64)
+        y_scales = keep.tile([P, QUERIES], U8, name="y_scales", align_bytes=64)
+        out_rows = out_0.rearrange("(p r) q -> p r q", r=PACK)
+        out_words = out_1[0].rearrange("p q u -> p (q u)").bitcast(I32)
+        def scores(u, o, bank, q_op):
+            codes, scale = q_op
+            for r in range(PACK):
+                nc.tensor.matmul_mx(
+                    out=bank[:, r, :],
+                    lhsT=k_code[o][:, 2 * P * r : 2 * P * (r + 1)].bitcast(FP4X4),
+                    lhsT_scale=k_scale[o][:, P * r : P * (r + 1)],
+                    rhs=codes[:].bitcast(FP8X4),
+                    rhs_scale=scale[:],
+                    start=(o == 0 and r == 0),
+                    stop=(o == PASSES - 1 and r == PACK - 1),
+                )
+
+        for chunk in range(QUERIES // CHUNK):
+            y = keep.tile([P, PACK, CHUNK], F32, name="y_%d" % chunk, align_bytes=64)
+            units = range(chunk * CHUNK // UNIT, (chunk + 1) * CHUNK // UNIT)
+            banks = {u: psum.tile([P, PACK, UNIT], F32, name="bank_%d" % u) for u in units}
+            for o in range(PASSES):
+                for u in units:
+                    if (u, o) not in q_ops:
+                        q_ops[u, o] = quantise_q(u, o)
+                    scores(u, o, banks[u], q_ops[u, o])
+            for u in units:
+                cols = slice(u * UNIT, (u + 1) * UNIT)
+                part = slice(cols.start - chunk * CHUNK, cols.stop - chunk * CHUNK)
+                shifted = keep.tile([P, PACK, UNIT], F32, name="shifted_%d" % u, align_bytes=64)
+                nc.vector.tensor_tensor(
+                    shifted[:], banks[u][:], ls_rows[:, cols].unsqueeze(1).to_broadcast([P, PACK, UNIT]), ALU.subtract
+                )
+                nc.scalar.activation(y[:, :, part], shifted[:], ACT.Exp)
+                if chunk == 1:
+                    nc.sync.dma_start(out_rows[:, :, cols], y[:, :, part])
+                elif u == units[-1]:
+                    nc.sync.dma_start(out_rows[:, :, chunk * CHUNK : (chunk + 1) * CHUNK], y[:])
+                y_grouped = keep.tile([P, UNIT, PACK], BF16, name="y_grouped_%d" % u, align_bytes=64)
+                interleave(nc.vector.tensor_copy, y_grouped[:], y[:, :, part])
+                nc.vector.quantize_mx(
+                    out=y_words[:, cols].bitcast(FP8X4),
+                    scales=y_scales[:, cols],
+                    in_=y_grouped[:].rearrange("p w t -> p (w t)"),
+                )
+            words = slice(chunk * CHUNK, (chunk + 1) * CHUNK)
+            nc.sync.dma_start(out_words[:, words], y_words[:, words])
+
+        out_scales = out_2[0].bitcast(I32)
+        for quad in range(4):
+            queue = nc.scalar if quad % 2 else nc.sync
+            queue.dma_start(
+                out_scales[4 * quad : 4 * quad + 4, :], y_scales[:].bitcast(I32)[32 * quad : 32 * quad + 4, :]
+            )

@@ -41,14 +41,8 @@ def tile_attend_plw_soft_kernel(tc, qT, k_words, k_scales, ls, offs, out_0, out_
         offsets = keep.tile([P, SLOTS // 16], U16, name="offsets")
         nc.sync.dma_start(offsets[:], offs)
 
-        ls_cols = keep.tile([P, 4], F32, name="ls_cols")
+        ls_cols = keep.tile([P, 4], F32, name="ls_cols", tag="q_grouped_0", align_bytes=64)
         nc.sync.dma_start(ls_cols[:], ls[0, 0].rearrange("(p j) -> p j", j=4))
-
-        scale_pool = keep.tile([P, POOL], U8, name="scale_pool", align_bytes=64)
-        nc.vector.memset(scale_pool[:].bitcast(I32), 0)
-        scale_rows = k_scales.bitcast(I32).rearrange("o (a i) t -> i a o t", i=4)
-        for i in range(4):
-            nc.sync.dma_start(scale_pool[:].bitcast(I32)[i:P:16, :], scale_rows[i])
 
         def load_q(chunk, o, tag):
             raw = keep.tile([P, PACK, CHUNK], F32, name="q_raw_%d_%d" % (chunk, o), tag=tag, align_bytes=64)
@@ -56,13 +50,21 @@ def tile_attend_plw_soft_kernel(tc, qT, k_words, k_scales, ls, offs, out_0, out_
             nc.sync.dma_start(raw[:], rows.rearrange("(p j) w -> p j w", j=PACK))
             return raw
 
-        q_raw = {}
-        q_raw[0, 0] = load_q(0, 0, "q_first")
         word_pool = keep.tile([P, POOL], I32, name="word_pool", align_bytes=64)
-        nc.sync.dma_start(word_pool[:], k_words[0].rearrange("p t b -> p (t b)").bitcast(I32))
+        pool_words = k_words[0].rearrange("p t b -> p (t b)").bitcast(I32)
+        nc.sync.dma_start(word_pool[:, : POOL // 2], pool_words[:, : POOL // 2])
+
+        scale_pool = keep.tile([P, POOL], U8, name="scale_pool", align_bytes=64)
+        nc.vector.memset(scale_pool[:].bitcast(I32), 0)
+        scale_rows = k_scales.bitcast(I32).rearrange("o (a i) t -> i a o t", i=4)
+        for i in range(4):
+            nc.sync.dma_start(scale_pool[:].bitcast(I32)[i:P:16, :], scale_rows[i])
+
+        nc.sync.dma_start(word_pool[:, POOL // 2 :], pool_words[:, POOL // 2 :])
+
+        q_raw = {(0, 0): load_q(0, 0, "q_first")}
         q_raw[0, 1] = load_q(0, 1, "q_second")
         q_raw[1, 0] = load_q(1, 0, "q_third")
-        q_raw[1, 1] = load_q(1, 1, "q_fourth")
 
         ident = keep.tile([P, P], F32, name="ident")
         make_identity(nc, ident[:])
@@ -74,38 +76,17 @@ def tile_attend_plw_soft_kernel(tc, qT, k_words, k_scales, ls, offs, out_0, out_
             ls_rows[:].rearrange("p (n j) -> p n j", j=4), ls_bank[:].rearrange("p j n -> p n j"), ACT.Copy
         )
 
-        on_vector = {(2, 1)}
-
-        def scalar_cast(dst, src):
-            nc.scalar.activation(dst, src, ACT.Copy)
-
-        def quantise_q(u, o):
-            chunk, part = divmod(u, CHUNK // UNIT)
-            grouped = keep.tile([P, UNIT, PACK], BF16, name="q_grouped_%d_%d" % (u, o), align_bytes=64)
-            copy = nc.vector.tensor_copy if (u, o) in on_vector else scalar_cast
-            interleave(copy, grouped[:], q_raw[chunk, o][:, :, part * UNIT : (part + 1) * UNIT])
-            codes = keep.tile([P, UNIT], U32, name="q_code_%d_%d" % (u, o), align_bytes=64)
-            scale = keep.tile([P, UNIT], U8, name="q_scale_%d_%d" % (u, o), align_bytes=64)
-            nc.vector.quantize_mx(
-                out=codes[:].bitcast(FP8X4), scales=scale[:], in_=grouped[:].rearrange("p w t -> p (w t)")
-            )
-            return codes, scale
-
-        q_ops = {(u, 0): quantise_q(u, 0) for u in range(CHUNK // UNIT)}
-
-        scales_listed = keep.tile([P, SLOTS], U8, name="scales_listed", align_bytes=64)
+        scales_listed = keep.tile([P, SLOTS], U8, name="scales_listed", tag="q_last", align_bytes=64)
         nc.vector.tensor_copy(scales_listed[:], scale_pool[:].indirect(offsets[:]))
-        k_scale = [
-            keep.tile([P, SLOTS], U8, name="k_scale_0", tag="q_first", align_bytes=64),
-            keep.tile([P, SLOTS], U8, name="k_scale_1", align_bytes=64),
-        ]
+        k_scale = [keep.tile([P, SLOTS], U8, name="k_scale_%d" % o, align_bytes=64) for o in range(PASSES)]
         nc.vector.tensor_copy(
             k_scale[0][:].rearrange("p (r c i) -> p c r i", r=PACK, i=16),
             scales_listed[:].rearrange("p (c i r) -> p c r i", r=PACK, i=16),
         )
         nc.gpsimd.memset(k_scale[1][:].bitcast(I32), 0)
         for i in range(4):
-            nc.scalar.dma_start(k_scale[1][:].bitcast(I32)[i:P:32, :], k_scale[0][:].bitcast(I32)[16 + i : P : 32, :])
+            nc.sync.dma_start(k_scale[1][:].bitcast(I32)[i:P:32, :], k_scale[0][:].bitcast(I32)[16 + i : P : 32, :])
+        q_raw[1, 1] = load_q(1, 1, "q_last")
 
         words_listed = keep.tile([P, SLOTS], U32, name="words_listed", align_bytes=64)
         nc.vector.tensor_copy(words_listed[:], word_pool[:].bitcast(U32).indirect(offsets[:]))
@@ -118,54 +99,116 @@ def tile_attend_plw_soft_kernel(tc, qT, k_words, k_scales, ls, offs, out_0, out_
             )
             k_code.append(codes)
 
-
+        q_grouped = [keep.tile([P, QUERIES, PACK], BF16, name="q_grouped_%d" % o, tag="q_grouped_%d" % o, align_bytes=64) for o in range(PASSES)]
+        q_code = [keep.tile([P, QUERIES], U32, name="q_code_%d" % o, align_bytes=64) for o in range(PASSES)]
+        q_scale = [keep.tile([P, QUERIES], U8, name="q_scale_%d" % o, align_bytes=64) for o in range(PASSES)]
+        banks = [psum.tile([P, PACK, UNIT], F32, name="bank_%d" % u) for u in range(QUERIES // UNIT)]
+        shifted = [keep.tile([P, PACK, CHUNK], F32, name="shifted_%d" % c, align_bytes=64) for c in range(QUERIES // CHUNK)]
+        y = [keep.tile([P, PACK, CHUNK], F32, name="y_%d" % c, align_bytes=64) for c in range(QUERIES // CHUNK)]
+        y_grouped = keep.tile([P, QUERIES, PACK], BF16, name="y_grouped", align_bytes=64)
         y_words = keep.tile([P, QUERIES], I32, name="y_words", align_bytes=64)
         y_scales = keep.tile([P, QUERIES], U8, name="y_scales", align_bytes=64)
         out_rows = out_0.rearrange("(p r) q -> p r q", r=PACK)
         out_words = out_1[0].rearrange("p q u -> p (q u)").bitcast(I32)
-        def scores(u, o, bank, q_op):
-            codes, scale = q_op
+
+        def columns(first, last):
+            return slice(first * UNIT, (last + 1) * UNIT)
+
+        def in_chunk(tiles, first, last):
+            chunk, part = divmod(first, CHUNK // UNIT)
+            return tiles[chunk][:, :, columns(part, part + last - first)]
+
+        def scalar_round(dst, src):
+            nc.scalar.activation(dst, src, ACT.Copy)
+
+        vector_round = nc.vector.tensor_copy
+
+        def round_q(copy, first, last, o):
+            raw = [q_raw[c, o] for c in range(QUERIES // CHUNK)]
+            interleave(copy, q_grouped[o][:, columns(first, last), :], in_chunk(raw, first, last))
+
+        def quantise_q(first, last, o):
+            cols = columns(first, last)
+            nc.vector.quantize_mx(
+                out=q_code[o][:, cols].bitcast(FP8X4),
+                scales=q_scale[o][:, cols],
+                in_=q_grouped[o][:, cols, :].rearrange("p w t -> p (w t)"),
+            )
+
+        def scores(u, o):
             for r in range(PACK):
                 nc.tensor.matmul_mx(
-                    out=bank[:, r, :],
+                    out=banks[u][:, r, :],
                     lhsT=k_code[o][:, 2 * P * r : 2 * P * (r + 1)].bitcast(FP4X4),
                     lhsT_scale=k_scale[o][:, P * r : P * (r + 1)],
-                    rhs=codes[:].bitcast(FP8X4),
-                    rhs_scale=scale[:],
+                    rhs=q_code[o][:, columns(u, u)].bitcast(FP8X4),
+                    rhs_scale=q_scale[o][:, columns(u, u)],
                     start=(o == 0 and r == 0),
                     stop=(o == PASSES - 1 and r == PACK - 1),
                 )
 
-        for chunk in range(QUERIES // CHUNK):
-            y = keep.tile([P, PACK, CHUNK], F32, name="y_%d" % chunk, align_bytes=64)
-            units = range(chunk * CHUNK // UNIT, (chunk + 1) * CHUNK // UNIT)
-            banks = {u: psum.tile([P, PACK, UNIT], F32, name="bank_%d" % u) for u in units}
-            for o in range(PASSES):
-                for u in units:
-                    if (u, o) not in q_ops:
-                        q_ops[u, o] = quantise_q(u, o)
-                    scores(u, o, banks[u], q_ops[u, o])
-            for u in units:
-                cols = slice(u * UNIT, (u + 1) * UNIT)
-                part = slice(cols.start - chunk * CHUNK, cols.stop - chunk * CHUNK)
-                shifted = keep.tile([P, PACK, UNIT], F32, name="shifted_%d" % u, align_bytes=64)
-                nc.vector.tensor_tensor(
-                    shifted[:], banks[u][:], ls_rows[:, cols].unsqueeze(1).to_broadcast([P, PACK, UNIT]), ALU.subtract
-                )
-                nc.scalar.activation(y[:, :, part], shifted[:], ACT.Exp)
-                if chunk == 1:
-                    nc.sync.dma_start(out_rows[:, :, cols], y[:, :, part])
-                elif u == units[-1]:
-                    nc.sync.dma_start(out_rows[:, :, chunk * CHUNK : (chunk + 1) * CHUNK], y[:])
-                y_grouped = keep.tile([P, UNIT, PACK], BF16, name="y_grouped_%d" % u, align_bytes=64)
-                interleave(nc.vector.tensor_copy, y_grouped[:], y[:, :, part])
-                nc.vector.quantize_mx(
-                    out=y_words[:, cols].bitcast(FP8X4),
-                    scales=y_scales[:, cols],
-                    in_=y_grouped[:].rearrange("p w t -> p (w t)"),
-                )
-            words = slice(chunk * CHUNK, (chunk + 1) * CHUNK)
-            nc.sync.dma_start(out_words[:, words], y_words[:, words])
+        def subtract_ls(u):
+            row = ls_rows[:, columns(u, u)].unsqueeze(1).to_broadcast([P, PACK, UNIT])
+            nc.vector.tensor_tensor(in_chunk(shifted, u, u), banks[u][:], row, ALU.subtract)
+
+        def weights(first, last):
+            nc.scalar.activation(in_chunk(y, first, last), in_chunk(shifted, first, last), ACT.Exp)
+
+        def store_weights(first, last):
+            nc.sync.dma_start(out_rows[:, :, columns(first, last)], in_chunk(y, first, last))
+
+        def round_y(copy, first, last):
+            interleave(copy, y_grouped[:, columns(first, last), :], in_chunk(y, first, last))
+
+        def quantise_y(first, last):
+            cols = columns(first, last)
+            nc.vector.quantize_mx(
+                out=y_words[:, cols].bitcast(FP8X4),
+                scales=y_scales[:, cols],
+                in_=y_grouped[:, cols, :].rearrange("p w t -> p (w t)"),
+            )
+
+        def store_words(first, last):
+            nc.sync.dma_start(out_words[:, columns(first, last)], y_words[:, columns(first, last)])
+
+        round_q(scalar_round, 0, 1, 0)
+        quantise_q(0, 1, 0)
+        scores(0, 0)
+        scores(1, 0)
+        round_q(scalar_round, 0, 0, 1)
+        round_q(vector_round, 1, 1, 1)
+        quantise_q(0, 0, 1)
+        scores(0, 1)
+        quantise_q(1, 1, 1)
+        scores(1, 1)
+        subtract_ls(0)
+        round_q(scalar_round, 2, 3, 0)
+        quantise_q(2, 3, 0)
+        scores(2, 0)
+        scores(3, 0)
+        subtract_ls(1)
+        round_q(scalar_round, 2, 2, 1)
+        round_q(vector_round, 3, 3, 1)
+        quantise_q(2, 2, 1)
+        scores(2, 1)
+        quantise_q(3, 3, 1)
+        scores(3, 1)
+        weights(0, 1)
+        store_weights(0, 1)
+        subtract_ls(2)
+        weights(2, 2)
+        subtract_ls(3)
+        weights(3, 3)
+        round_y(vector_round, 0, 1)
+        quantise_y(0, 1)
+        store_words(0, 1)
+        store_weights(2, 2)
+        round_y(vector_round, 2, 2)
+        quantise_y(2, 2)
+        store_weights(3, 3)
+        round_y(vector_round, 3, 3)
+        quantise_y(3, 3)
+        store_words(2, 3)
 
         out_scales = out_2[0].bitcast(I32)
         for quad in range(4):

@@ -20,8 +20,9 @@ PASSES = 2
 SLOTS = 512
 POOL = 2048
 QUERIES = 512
-UNIT = 128
 CHUNK = 256
+BLOCK = 128
+QUAD = 32
 FLOPS = 2 * PASSES * P * PACK * SLOTS * QUERIES
 
 
@@ -38,181 +39,187 @@ def tile_attend_plw_soft_kernel(tc, qT, k_words, k_scales, ls, offs, out_0, out_
         keep = ctx.enter_context(tc.tile_pool(name="keep", bufs=1))
         psum = ctx.enter_context(tc.psum_pool(name="psum", bufs=1))
 
+        def sbuf(name, shape, dtype, bytes_of=None):
+            return keep.tile(shape, dtype, name=name, tag=bytes_of or name, align_bytes=64)
+
         offsets = keep.tile([P, SLOTS // 16], U16, name="offsets")
         nc.sync.dma_start(offsets[:], offs)
 
-        ls_cols = keep.tile([P, 4], F32, name="ls_cols", tag="q_grouped_0", align_bytes=64)
+        ls_cols = sbuf("ls_cols", [P, 4], F32)
         nc.sync.dma_start(ls_cols[:], ls[0, 0].rearrange("(p j) -> p j", j=4))
 
-        def load_q(chunk, o, tag):
-            raw = keep.tile([P, PACK, CHUNK], F32, name="q_raw_%d_%d" % (chunk, o), tag=tag, align_bytes=64)
-            rows = qT[0, o * P * PACK : (o + 1) * P * PACK, chunk * CHUNK : (chunk + 1) * CHUNK]
-            nc.sync.dma_start(raw[:], rows.rearrange("(p j) w -> p j w", j=PACK))
-            return raw
-
-        word_pool = keep.tile([P, POOL], I32, name="word_pool", align_bytes=64)
+        word_pool = sbuf("word_pool", [P, POOL], I32)
         pool_words = k_words[0].rearrange("p t b -> p (t b)").bitcast(I32)
         nc.sync.dma_start(word_pool[:, : POOL // 2], pool_words[:, : POOL // 2])
 
-        scale_pool = keep.tile([P, POOL], U8, name="scale_pool", align_bytes=64)
+        scale_pool = sbuf("scale_pool", [P, POOL], U8)
         nc.vector.memset(scale_pool[:].bitcast(I32), 0)
         scale_rows = k_scales.bitcast(I32).rearrange("o (a i) t -> i a o t", i=4)
         for i in range(4):
-            nc.sync.dma_start(scale_pool[:].bitcast(I32)[i:P:16, :], scale_rows[i])
+            nc.sync.dma_start(scale_pool[:].bitcast(I32)[i : P : QUAD // 2, :], scale_rows[i])
 
         nc.sync.dma_start(word_pool[:, POOL // 2 :], pool_words[:, POOL // 2 :])
 
-        q_raw = {(0, 0): load_q(0, 0, "q_first")}
-        q_raw[0, 1] = load_q(0, 1, "q_second")
-        q_raw[1, 0] = load_q(1, 0, "q_third")
+        def load_q(chunk, o, bytes_of=None):
+            raw = sbuf("q_raw_%d_%d" % (chunk, o), [P, PACK, CHUNK], F32, bytes_of)
+            rows = qT[0, o * P * PACK : (o + 1) * P * PACK, chunk * CHUNK : (chunk + 1) * CHUNK]
+            nc.sync.dma_start(raw[:], rows.rearrange("(p t) w -> p t w", t=PACK))
+            return raw
 
-        ident = keep.tile([P, P], F32, name="ident")
+        q_raw = {(chunk, o): load_q(chunk, o) for chunk, o in ((0, 0), (0, 1), (1, 0))}
+
+        ident = sbuf("ident", [P, P], F32)
         make_identity(nc, ident[:])
         ls_bank = psum.tile([P, 4, P], F32, name="ls_bank")
         for j in range(4):
             nc.tensor.transpose(ls_bank[:, j, :], ls_cols[:, j : j + 1].to_broadcast([P, P]), ident[:])
-        ls_rows = keep.tile([P, QUERIES], F32, name="ls_rows")
+        ls_rows = sbuf("ls_rows", [P, QUERIES], F32)
         nc.scalar.activation(
             ls_rows[:].rearrange("p (n j) -> p n j", j=4), ls_bank[:].rearrange("p j n -> p n j"), ACT.Copy
         )
 
-        scales_listed = keep.tile([P, SLOTS], U8, name="scales_listed", tag="q_last", align_bytes=64)
+        scales_listed = sbuf("scales_listed", [P, SLOTS], U8)
         nc.vector.tensor_copy(scales_listed[:], scale_pool[:].indirect(offsets[:]))
-        k_scale = [keep.tile([P, SLOTS], U8, name="k_scale_%d" % o, align_bytes=64) for o in range(PASSES)]
+        k_scale = [sbuf("k_scale_%d" % o, [P, SLOTS], U8) for o in range(PASSES)]
         nc.vector.tensor_copy(
             k_scale[0][:].rearrange("p (r c i) -> p c r i", r=PACK, i=16),
             scales_listed[:].rearrange("p (c i r) -> p c r i", r=PACK, i=16),
         )
         nc.gpsimd.memset(k_scale[1][:].bitcast(I32), 0)
         for i in range(4):
-            nc.sync.dma_start(k_scale[1][:].bitcast(I32)[i:P:32, :], k_scale[0][:].bitcast(I32)[16 + i : P : 32, :])
-        q_raw[1, 1] = load_q(1, 1, "q_last")
-
-        words_listed = keep.tile([P, SLOTS], U32, name="words_listed", align_bytes=64)
-        nc.vector.tensor_copy(words_listed[:], word_pool[:].bitcast(U32).indirect(offsets[:]))
-        k_code = []
-        for o in range(PASSES):
-            codes = keep.tile([P, 2 * SLOTS], U8, name="k_code_%d" % o, align_bytes=64)
-            nc.vector.tensor_copy(
-                codes[:].bitcast(U16).rearrange("p (r c i) -> p c r i", r=PACK, i=4),
-                words_listed[:].bitcast(U16).rearrange("p (c i r h) -> p h c r i", r=PACK, i=4, h=PASSES)[:, o],
+            nc.sync.dma_start(
+                k_scale[1][:].bitcast(I32)[i:P:QUAD, :], k_scale[0][:].bitcast(I32)[QUAD // 2 + i : P : QUAD, :]
             )
-            k_code.append(codes)
+        q_raw[1, 1] = load_q(1, 1, "scales_listed")
 
-        q_grouped = [keep.tile([P, QUERIES, PACK], BF16, name="q_grouped_%d" % o, tag="q_grouped_%d" % o, align_bytes=64) for o in range(PASSES)]
-        q_code = [keep.tile([P, QUERIES], U32, name="q_code_%d" % o, align_bytes=64) for o in range(PASSES)]
-        q_scale = [keep.tile([P, QUERIES], U8, name="q_scale_%d" % o, align_bytes=64) for o in range(PASSES)]
-        banks = [psum.tile([P, PACK, UNIT], F32, name="bank_%d" % u) for u in range(QUERIES // UNIT)]
-        shifted = [keep.tile([P, PACK, CHUNK], F32, name="shifted_%d" % c, align_bytes=64) for c in range(QUERIES // CHUNK)]
-        y = [keep.tile([P, PACK, CHUNK], F32, name="y_%d" % c, align_bytes=64) for c in range(QUERIES // CHUNK)]
-        y_grouped = keep.tile([P, QUERIES, PACK], BF16, name="y_grouped", align_bytes=64)
-        y_words = keep.tile([P, QUERIES], I32, name="y_words", align_bytes=64)
-        y_scales = keep.tile([P, QUERIES], U8, name="y_scales", align_bytes=64)
+        words_listed = sbuf("words_listed", [P, SLOTS], U32)
+        nc.vector.tensor_copy(words_listed[:], word_pool[:].bitcast(U32).indirect(offsets[:]))
+
+        chunks = range(QUERIES // CHUNK)
+        banks = [psum.tile([P, PACK, BLOCK], F32, name="bank_%d" % b) for b in range(QUERIES // BLOCK)]
+        shifted = [sbuf("shifted_%d" % chunk, [P, PACK, CHUNK], F32) for chunk in chunks]
+        y = [sbuf("y_%d" % chunk, [P, PACK, CHUNK], F32) for chunk in chunks]
+        y_rounded = sbuf("y_rounded", [P, QUERIES, PACK], BF16)
+        y_words = sbuf("y_words", [P, QUERIES], I32)
+        y_scales = sbuf("y_scales", [P, QUERIES], U8)
         out_rows = out_0.rearrange("(p r) q -> p r q", r=PACK)
         out_words = out_1[0].rearrange("p q u -> p (q u)").bitcast(I32)
 
         def columns(first, last):
-            return slice(first * UNIT, (last + 1) * UNIT)
+            return slice(first * BLOCK, (last + 1) * BLOCK)
 
         def in_chunk(tiles, first, last):
-            chunk, part = divmod(first, CHUNK // UNIT)
+            chunk, part = divmod(first, CHUNK // BLOCK)
             return tiles[chunk][:, :, columns(part, part + last - first)]
 
-        def scalar_round(dst, src):
+        own_tile = {(0, 0): "ls_cols", (1, 1): "q_raw_0_0", (3, 1): "q_code_0_1"}
+        one_tile = [(1, 0), (0, 1), (2, 0), (3, 0), (2, 1)]
+        by_scalar = sbuf("by_scalar", [P, len(one_tile) * BLOCK, PACK], BF16, "ident")
+        q_rounded = {}
+        q_planes = {}
+
+        def scalar_copy(dst, src):
             nc.scalar.activation(dst, src, ACT.Copy)
 
-        vector_round = nc.vector.tensor_copy
+        def round_q(b, o):
+            if (b, o) in own_tile:
+                rounded = sbuf("q_rounded_%d_%d" % (b, o), [P, BLOCK, PACK], BF16, own_tile[b, o])[:]
+            else:
+                place = one_tile.index((b, o))
+                rounded = by_scalar[:, columns(place, place), :]
+            copy = nc.vector.tensor_copy if o == 1 and b % 2 == 1 else scalar_copy
+            interleave(copy, rounded, in_chunk([q_raw[chunk, o] for chunk in chunks], b, b))
+            q_rounded[b, o] = rounded
 
-        def round_q(copy, first, last, o):
-            raw = [q_raw[c, o] for c in range(QUERIES // CHUNK)]
-            interleave(copy, q_grouped[o][:, columns(first, last), :], in_chunk(raw, first, last))
-
-        def quantise_q(first, last, o):
-            cols = columns(first, last)
+        def quantise_q(b, o):
+            codes = sbuf("q_code_%d_%d" % (b, o), [P, BLOCK], U32)
+            scale = sbuf("q_scale_%d_%d" % (b, o), [P, BLOCK], U8)
             nc.vector.quantize_mx(
-                out=q_code[o][:, cols].bitcast(FP8X4),
-                scales=q_scale[o][:, cols],
-                in_=q_grouped[o][:, cols, :].rearrange("p w t -> p (w t)"),
+                out=codes[:].bitcast(FP8X4), scales=scale[:], in_=q_rounded[b, o].rearrange("p w t -> p (w t)")
             )
+            q_planes[b, o] = (codes, scale)
 
-        def scores(u, o):
+        def multiply(b, o):
+            codes, scale = q_planes[b, o]
             for r in range(PACK):
+                first = o * SLOTS + r * P
                 nc.tensor.matmul_mx(
-                    out=banks[u][:, r, :],
-                    lhsT=k_code[o][:, 2 * P * r : 2 * P * (r + 1)].bitcast(FP4X4),
-                    lhsT_scale=k_scale[o][:, P * r : P * (r + 1)],
-                    rhs=q_code[o][:, columns(u, u)].bitcast(FP8X4),
-                    rhs_scale=q_scale[o][:, columns(u, u)],
+                    out=banks[b][:, r, :],
+                    lhsT=k_code[:, 2 * first : 2 * (first + P)].bitcast(FP4X4),
+                    lhsT_scale=k_scale[o][:, r * P : (r + 1) * P],
+                    rhs=codes[:].bitcast(FP8X4),
+                    rhs_scale=scale[:],
                     start=(o == 0 and r == 0),
                     stop=(o == PASSES - 1 and r == PACK - 1),
                 )
 
-        def subtract_ls(u):
-            row = ls_rows[:, columns(u, u)].unsqueeze(1).to_broadcast([P, PACK, UNIT])
-            nc.vector.tensor_tensor(in_chunk(shifted, u, u), banks[u][:], row, ALU.subtract)
+        def scores(b, o):
+            quantise_q(b, o)
+            multiply(b, o)
 
-        def weights(first, last):
-            nc.scalar.activation(in_chunk(y, first, last), in_chunk(shifted, first, last), ACT.Exp)
+        def subtract_ls(b):
+            row = ls_rows[:, columns(b, b)].unsqueeze(1).to_broadcast([P, PACK, BLOCK])
+            nc.vector.tensor_tensor(in_chunk(shifted, b, b), banks[b][:], row, ALU.subtract)
 
-        def store_weights(first, last):
+        def exp(b):
+            nc.scalar.activation(in_chunk(y, b, b), in_chunk(shifted, b, b), ACT.Exp)
+
+        def store_y(first, last):
             nc.sync.dma_start(out_rows[:, :, columns(first, last)], in_chunk(y, first, last))
 
-        def round_y(copy, first, last):
-            interleave(copy, y_grouped[:, columns(first, last), :], in_chunk(y, first, last))
+        def round_y(first, last):
+            interleave(nc.vector.tensor_copy, y_rounded[:, columns(first, last), :], in_chunk(y, first, last))
 
-        def quantise_y(first, last):
+        def planes(first, last):
             cols = columns(first, last)
             nc.vector.quantize_mx(
                 out=y_words[:, cols].bitcast(FP8X4),
                 scales=y_scales[:, cols],
-                in_=y_grouped[:, cols, :].rearrange("p w t -> p (w t)"),
+                in_=y_rounded[:, cols, :].rearrange("p w t -> p (w t)"),
             )
+            nc.sync.dma_start(out_words[:, cols], y_words[:, cols])
 
-        def store_words(first, last):
-            nc.sync.dma_start(out_words[:, columns(first, last)], y_words[:, columns(first, last)])
-
-        round_q(scalar_round, 0, 1, 0)
-        quantise_q(0, 1, 0)
-        scores(0, 0)
+        round_q(0, 0)
+        quantise_q(0, 0)
+        k_code = sbuf("k_code", [P, PASSES * SLOTS * 2], U8, "ls_cols")
+        nc.vector.tensor_copy(
+            k_code[:].bitcast(U16).rearrange("p (o r c i) -> p o c r i", o=PASSES, r=PACK, i=4),
+            words_listed[:].bitcast(U16).rearrange("p (c i r o) -> p o c r i", o=PASSES, r=PACK, i=4),
+        )
+        multiply(0, 0)
+        round_q(1, 0)
         scores(1, 0)
-        round_q(scalar_round, 0, 0, 1)
-        round_q(vector_round, 1, 1, 1)
-        quantise_q(0, 0, 1)
+        round_q(0, 1)
+        round_q(1, 1)
         scores(0, 1)
-        quantise_q(1, 1, 1)
         scores(1, 1)
-        subtract_ls(0)
-        round_q(scalar_round, 2, 3, 0)
-        quantise_q(2, 3, 0)
+
+        round_q(2, 0)
         scores(2, 0)
+        subtract_ls(0)
+        round_q(3, 0)
         scores(3, 0)
-        subtract_ls(1)
-        round_q(scalar_round, 2, 2, 1)
-        round_q(vector_round, 3, 3, 1)
-        quantise_q(2, 2, 1)
-        scores(2, 1)
-        quantise_q(3, 3, 1)
+        round_q(2, 1)
+        round_q(3, 1)
         scores(3, 1)
-        weights(0, 1)
-        store_weights(0, 1)
-        subtract_ls(2)
-        weights(2, 2)
-        subtract_ls(3)
-        weights(3, 3)
-        round_y(vector_round, 0, 1)
-        quantise_y(0, 1)
-        store_words(0, 1)
-        store_weights(2, 2)
-        round_y(vector_round, 2, 2)
-        quantise_y(2, 2)
-        store_weights(3, 3)
-        round_y(vector_round, 3, 3)
-        quantise_y(3, 3)
-        store_words(2, 3)
+        scores(2, 1)
+
+        exp(0)
+        subtract_ls(1)
+        exp(1)
+        store_y(0, 1)
+        for b in (3, 2):
+            subtract_ls(b)
+            exp(b)
+        round_y(0, 1)
+        store_y(3, 3)
+        round_y(3, 3)
+        planes(0, 1)
+        store_y(2, 2)
+        round_y(2, 2)
+        planes(2, 3)
 
         out_scales = out_2[0].bitcast(I32)
-        for quad in range(4):
-            queue = nc.scalar if quad % 2 else nc.sync
-            queue.dma_start(
-                out_scales[4 * quad : 4 * quad + 4, :], y_scales[:].bitcast(I32)[32 * quad : 32 * quad + 4, :]
-            )
+        for a in range(P // QUAD):
+            queue = nc.scalar if a % 2 else nc.sync
+            queue.dma_start(out_scales[4 * a : 4 * a + 4, :], y_scales[:].bitcast(I32)[QUAD * a : QUAD * a + 4, :])

from contextlib import ExitStack

import concourse.mybir as mybir
from concourse.masks import make_identity

F32 = mybir.dt.float32
BF16 = mybir.dt.bfloat16
I32 = mybir.dt.int32
U32 = mybir.dt.uint32
U16 = mybir.dt.uint16
U8 = mybir.dt.uint8
FP8X4 = mybir.dt.float8_e4m3fn_x4
FP4X4 = mybir.dt.float4_e2m1fn_x4
ACT = mybir.ActivationFunctionType
ALU = mybir.AluOpType

P = 128
PACK = 4
PASSES = 2
SLOTS = 512
POOL = 2048
QUERIES = 512
CHUNK = 256
BLOCK = 128
QUAD = 32
FLOPS = 2 * PASSES * P * PACK * SLOTS * QUERIES


def interleave(copy, dst, src):
    copy(
        dst.rearrange("p (c i) t -> p c t i", i=4),
        src.rearrange("p t (c i) -> p c t i", i=4),
    )


def tile_attend_plw_soft_kernel(tc, qT, k_words, k_scales, ls, offs, out_0, out_1, out_2):
    nc = tc.nc
    with ExitStack() as ctx:
        keep = ctx.enter_context(tc.tile_pool(name="keep", bufs=1))
        psum = ctx.enter_context(tc.psum_pool(name="psum", bufs=1))

        def sbuf(name, shape, dtype, bytes_of=None):
            return keep.tile(shape, dtype, name=name, tag=bytes_of or name, align_bytes=64)

        offsets = keep.tile([P, SLOTS // 16], U16, name="offsets")
        nc.sync.dma_start(offsets[:], offs)

        ls_cols = sbuf("ls_cols", [P, 4], F32)
        nc.sync.dma_start(ls_cols[:], ls[0, 0].rearrange("(p j) -> p j", j=4))

        word_pool = sbuf("word_pool", [P, POOL], I32)
        pool_words = k_words[0].rearrange("p t b -> p (t b)").bitcast(I32)
        nc.sync.dma_start(word_pool[:, : POOL // 2], pool_words[:, : POOL // 2])

        scale_pool = sbuf("scale_pool", [P, POOL], U8)
        nc.vector.memset(scale_pool[:].bitcast(I32), 0)
        scale_rows = k_scales.bitcast(I32).rearrange("o (a i) t -> i a o t", i=4)
        for i in range(4):
            nc.sync.dma_start(scale_pool[:].bitcast(I32)[i : P : QUAD // 2, :], scale_rows[i])

        nc.sync.dma_start(word_pool[:, POOL // 2 :], pool_words[:, POOL // 2 :])

        def load_q(chunk, o, bytes_of=None):
            raw = sbuf("q_raw_%d_%d" % (chunk, o), [P, PACK, CHUNK], F32, bytes_of)
            rows = qT[0, o * P * PACK : (o + 1) * P * PACK, chunk * CHUNK : (chunk + 1) * CHUNK]
            nc.sync.dma_start(raw[:], rows.rearrange("(p t) w -> p t w", t=PACK))
            return raw

        q_raw = {(chunk, o): load_q(chunk, o) for chunk, o in ((0, 0), (0, 1), (1, 0))}

        ident = sbuf("ident", [P, P], F32)
        make_identity(nc, ident[:])
        ls_bank = psum.tile([P, 4, P], F32, name="ls_bank")
        for j in range(4):
            nc.tensor.transpose(ls_bank[:, j, :], ls_cols[:, j : j + 1].to_broadcast([P, P]), ident[:])
        ls_rows = sbuf("ls_rows", [P, QUERIES], F32)
        nc.scalar.activation(
            ls_rows[:].rearrange("p (n j) -> p n j", j=4), ls_bank[:].rearrange("p j n -> p n j"), ACT.Copy
        )

        scales_listed = sbuf("scales_listed", [P, SLOTS], U8)
        nc.vector.tensor_copy(scales_listed[:], scale_pool[:].indirect(offsets[:]))
        k_scale = [sbuf("k_scale_%d" % o, [P, SLOTS], U8) for o in range(PASSES)]
        nc.vector.tensor_copy(
            k_scale[0][:].rearrange("p (r c i) -> p c r i", r=PACK, i=16),
            scales_listed[:].rearrange("p (c i r) -> p c r i", r=PACK, i=16),
        )
        nc.gpsimd.memset(k_scale[1][:].bitcast(I32), 0)
        for i in range(4):
            nc.sync.dma_start(
                k_scale[1][:].bitcast(I32)[i:P:QUAD, :], k_scale[0][:].bitcast(I32)[QUAD // 2 + i : P : QUAD, :]
            )
        q_raw[1, 1] = load_q(1, 1, "scales_listed")

        words_listed = sbuf("words_listed", [P, SLOTS], U32)
        nc.vector.tensor_copy(words_listed[:], word_pool[:].bitcast(U32).indirect(offsets[:]))

        chunks = range(QUERIES // CHUNK)
        banks = [psum.tile([P, PACK, BLOCK], F32, name="bank_%d" % b) for b in range(QUERIES // BLOCK)]
        shifted = [sbuf("shifted_%d" % chunk, [P, PACK, CHUNK], F32) for chunk in chunks]
        y = [sbuf("y_%d" % chunk, [P, PACK, CHUNK], F32) for chunk in chunks]
        y_rounded = sbuf("y_rounded", [P, QUERIES, PACK], BF16)
        y_words = sbuf("y_words", [P, QUERIES], I32)
        y_scales = sbuf("y_scales", [P, QUERIES], U8)
        out_rows = out_0.rearrange("(p r) q -> p r q", r=PACK)
        out_words = out_1[0].rearrange("p q u -> p (q u)").bitcast(I32)

        def columns(first, last):
            return slice(first * BLOCK, (last + 1) * BLOCK)

        def in_chunk(tiles, first, last):
            chunk, part = divmod(first, CHUNK // BLOCK)
            return tiles[chunk][:, :, columns(part, part + last - first)]

        own_tile = {(0, 0): "ls_cols", (1, 1): "q_raw_0_0", (3, 1): "q_code_0_1"}
        one_tile = [(1, 0), (0, 1), (2, 0), (3, 0), (2, 1)]
        by_scalar = sbuf("by_scalar", [P, len(one_tile) * BLOCK, PACK], BF16, "ident")
        q_rounded = {}
        q_planes = {}

        def scalar_copy(dst, src):
            nc.scalar.activation(dst, src, ACT.Copy)

        def round_q(b, o):
            if (b, o) in own_tile:
                rounded = sbuf("q_rounded_%d_%d" % (b, o), [P, BLOCK, PACK], BF16, own_tile[b, o])[:]
            else:
                place = one_tile.index((b, o))
                rounded = by_scalar[:, columns(place, place), :]
            copy = nc.vector.tensor_copy if o == 1 and b % 2 == 1 else scalar_copy
            interleave(copy, rounded, in_chunk([q_raw[chunk, o] for chunk in chunks], b, b))
            q_rounded[b, o] = rounded

        def quantise_q(b, o):
            codes = sbuf("q_code_%d_%d" % (b, o), [P, BLOCK], U32)
            scale = sbuf("q_scale_%d_%d" % (b, o), [P, BLOCK], U8)
            nc.vector.quantize_mx(
                out=codes[:].bitcast(FP8X4), scales=scale[:], in_=q_rounded[b, o].rearrange("p w t -> p (w t)")
            )
            q_planes[b, o] = (codes, scale)

        def multiply(b, o):
            codes, scale = q_planes[b, o]
            for r in range(PACK):
                first = o * SLOTS + r * P
                nc.tensor.matmul_mx(
                    out=banks[b][:, r, :],
                    lhsT=k_code[:, 2 * first : 2 * (first + P)].bitcast(FP4X4),
                    lhsT_scale=k_scale[o][:, r * P : (r + 1) * P],
                    rhs=codes[:].bitcast(FP8X4),
                    rhs_scale=scale[:],
                    start=(o == 0 and r == 0),
                    stop=(o == PASSES - 1 and r == PACK - 1),
                )

        def scores(b, o):
            quantise_q(b, o)
            multiply(b, o)

        def subtract_ls(b):
            row = ls_rows[:, columns(b, b)].unsqueeze(1).to_broadcast([P, PACK, BLOCK])
            nc.vector.tensor_tensor(in_chunk(shifted, b, b), banks[b][:], row, ALU.subtract)

        def exp(b):
            nc.scalar.activation(in_chunk(y, b, b), in_chunk(shifted, b, b), ACT.Exp)

        def store_y(first, last):
            nc.sync.dma_start(out_rows[:, :, columns(first, last)], in_chunk(y, first, last))

        def round_y(first, last):
            interleave(nc.vector.tensor_copy, y_rounded[:, columns(first, last), :], in_chunk(y, first, last))

        def planes(first, last):
            cols = columns(first, last)
            nc.vector.quantize_mx(
                out=y_words[:, cols].bitcast(FP8X4),
                scales=y_scales[:, cols],
                in_=y_rounded[:, cols, :].rearrange("p w t -> p (w t)"),
            )
            nc.sync.dma_start(out_words[:, cols], y_words[:, cols])

        round_q(0, 0)
        quantise_q(0, 0)
        k_code = sbuf("k_code", [P, PASSES * SLOTS * 2], U8, "ls_cols")
        nc.vector.tensor_copy(
            k_code[:].bitcast(U16).rearrange("p (o r c i) -> p o c r i", o=PASSES, r=PACK, i=4),
            words_listed[:].bitcast(U16).rearrange("p (c i r o) -> p o c r i", o=PASSES, r=PACK, i=4),
        )
        multiply(0, 0)
        round_q(1, 0)
        scores(1, 0)
        round_q(0, 1)
        round_q(1, 1)
        scores(0, 1)
        scores(1, 1)

        round_q(2, 0)
        scores(2, 0)
        subtract_ls(0)
        round_q(3, 0)
        scores(3, 0)
        round_q(2, 1)
        round_q(3, 1)
        scores(3, 1)
        scores(2, 1)

        exp(0)
        subtract_ls(1)
        exp(1)
        store_y(0, 1)
        for b in (3, 2):
            subtract_ls(b)
            exp(b)
        round_y(0, 1)
        store_y(3, 3)
        round_y(3, 3)
        planes(0, 1)
        store_y(2, 2)
        round_y(2, 2)
        planes(2, 3)

        out_scales = out_2[0].bitcast(I32)
        for a in range(P // QUAD):
            queue = nc.scalar if a % 2 else nc.sync
            queue.dma_start(out_scales[4 * a : 4 * a + 4, :], y_scales[:].bitcast(I32)[QUAD * a : QUAD * a + 4, :])
